import numpy as np
import ml_dtypes


def mxq(x, axis, fmt="e4m3"):
    dtype, down = {"e4m3": (ml_dtypes.float8_e4m3fn, 7), "e5m2": (ml_dtypes.float8_e5m2, 14)}[fmt]
    v = np.moveaxis(np.asarray(x, np.float32).astype(ml_dtypes.bfloat16).astype(np.float64), axis, -1)
    blocks = v.reshape(v.shape[:-1] + (-1, 32))
    amax = np.abs(blocks).max(-1, keepdims=True)
    byte = np.maximum(np.where(amax > 0, np.frexp(amax)[1] - 1 + 127, 0) - down, 1)
    scale = np.exp2(byte - 127.0)
    codes = (blocks / scale).astype(np.float32).astype(dtype).astype(np.float64)
    return np.moveaxis((codes * scale).reshape(v.shape), -1, axis)


WIDE = False


def mx_kscale(k):
    if not WIDE:
        return np.ones(k)
    levels = np.array([10, -10, 5, -5, 0])
    if k % 512:
        return np.exp2(np.random.permutation(np.resize(levels, k // 32))).repeat(32)
    a = np.empty((k // 512, 16))
    for p in range(k // 512):
        a[p, :8] = np.random.permutation(np.resize(levels, 8))
        for g in range(8):
            far = levels[np.abs(levels - a[p, g]) >= 10]
            a[p, g + 8] = far[np.random.randint(len(far))]
    return np.exp2(a.ravel()).repeat(32)


def f64(x):
    return np.asarray(x).astype(np.float64)


def striped(idx):
    return np.tile(idx.reshape(-1, 16).T, (8, 1)).astype(np.uint16)


def unstriped(offs):
    return offs[:16].T.reshape(-1).astype(np.int64)


def striped8(idx):
    return np.concatenate([x.reshape(-1, 16).T for x in idx]).astype(np.uint16)


def runs(offs, k):
    lists = np.stack([offs[16 * r : 16 * r + 16].T.reshape(-1) for r in range(8)]).astype(np.int64)
    return lists[np.arange(k) % 512 // 64]


def pack_weight(w):
    k, n = w.shape
    w = f64(np.asarray(w, np.float32).astype(ml_dtypes.bfloat16)).reshape(k // 32, 32, n)
    amax = np.abs(w).max(1)
    byte = np.clip(np.where(amax > 0, np.frexp(amax)[1] - 1 + 127 - 7, 1), 1, 254)
    scaled = (w * np.exp2(127.0 - byte)[:, None, :]).reshape(k, n).astype(np.float32)
    words = np.ascontiguousarray(scaled.reshape(k // 512, 128, 4, n).transpose(0, 1, 3, 2)).astype(ml_dtypes.float8_e4m3fn).view(np.uint8)
    return words, np.ascontiguousarray(byte.astype(np.uint8).reshape(k // 512, 16, n))


def unpack_weight(words, scales):
    g, p, n, _ = words.shape
    vals = np.ascontiguousarray(words).view(ml_dtypes.float8_e4m3fn).astype(np.float64) * np.repeat(np.exp2(scales.astype(np.float64) - 127.0), 8, axis=1)[..., None]
    return vals.transpose(0, 1, 3, 2).reshape(g * 512, n)


def relu(v):
    return np.maximum(v, 0.0)


K, T, S, N, H, W = 512, 2048, 512, 512, 512, 2048


def setup_inputs():
    n = np.random.standard_normal
    s = mx_kscale(K)[:, None]
    u = mx_kscale(H)
    packed_xT = pack_weight(n((K, T)) * s)
    return {
        "x_words": packed_xT[0],
        "x_scales": packed_xT[1],
        "w1": (n((K, H)) / np.sqrt(K) / s).astype(np.float32),
        "gn": (np.random.uniform(0.5, 1.5, (H, 1)) * u[:, None]).astype(np.float32),
        "w2": (n((H, N)) / np.sqrt(2 * H) / u[:, None]).astype(np.float32),
        "w3": (n((K, N)) / np.sqrt(2 * K) / s).astype(np.float32),
        "offs": striped(np.random.permutation(T)[:S]),
        "n1": striped(np.random.randint(0, S, W)),
        "two": striped(np.random.permutation(T)[:S]),
        "n2": striped8(np.stack([np.random.permutation(S) for _ in range(8)])),
        "n3": striped8(np.stack([np.random.permutation(S) for _ in range(8)])),
    }


def reference(x_words, x_scales, w1, gn, w2, w3, offs, n1, two, n2, n3):
    xq = unpack_weight(x_words, x_scales)[:, unstriped(offs)]
    y = mxq(f64(w1), 0, "e4m3").T @ xq
    ex = np.exp(0.5 * y)
    mb = ex[:, unstriped(n1)]
    ms = mb.reshape(H, S, 4).sum(axis=2)
    z = f64(gn) * ((4.0 * ex) / (ms + 0.5))
    x_two = unpack_weight(x_words, x_scales)[:, unstriped(two)]
    h = mxq(f64(w2), 0, "e4m3").T @ mxq(z, 0, "e4m3") + mxq(f64(w3), 0, "e4m3").T @ x_two
    return relu(h - (h[np.arange(N)[:, None], runs(n2, N)])) + 0.5 * (relu(h[np.arange(N)[:, None], runs(n3, N)] - h))

@@ -1,0 +1,233 @@
+from contextlib import ExitStack
+
+import concourse.mybir as mybir
+
+F32 = mybir.dt.float32
+BF16 = mybir.dt.bfloat16
+I32 = mybir.dt.int32
+U32 = mybir.dt.uint32
+U16 = mybir.dt.uint16
+U8 = mybir.dt.uint8
+FP8X4 = mybir.dt.float8_e4m3fn_x4
+ALU = mybir.AluOpType
+ACT = mybir.ActivationFunctionType
+
+P = 128
+PACK = 4
+K, T, S, H, N = 512, 2048, 512, 512, 512
+MEMBERS = 4
+CHUNK = 128
+CHUNKS = S // CHUNK
+SPARE = 32
+HALF = S // 2
+W1_SPLIT = 384
+FLOPS = 3 * 2 * 512 * 512 * 512
+
+
+def tile_picked_mixingsharehinge_none_p_kernel(tc, x_words, x_scales, w1, gn, w2, w3, offs, n1, two, n2, n3, out):
+    nc = tc.nc
+
+    def gather(engine, dst, window, offsets):
+        if engine == "vector":
+            nc.vector.tensor_copy(dst, window.indirect(offsets))
+        else:
+            nc.scalar.activation(dst, window.indirect(offsets), ACT.Copy)
+
+    def weave(engine, grouped, raw, m0, m1, raw_m0):
+        dst = grouped[:].rearrange("p (t m j) -> p m t j", t=PACK, j=PACK)[:, m0:m1]
+        src = raw[:].rearrange("p j (m t) -> p m t j", t=PACK)[:, m0 - raw_m0 : m1 - raw_m0]
+        if engine == "vector":
+            nc.vector.tensor_copy(dst, src)
+        else:
+            nc.scalar.activation(dst, src, ACT.Copy)
+
+    with ExitStack() as ctx:
+        lists = ctx.enter_context(tc.tile_pool(name="lists", bufs=1))
+        keep = ctx.enter_context(tc.tile_pool(name="keep", bufs=1))
+        psum = ctx.enter_context(tc.psum_pool(name="psum", bufs=1))
+
+        offs_sb = lists.tile([P, S // 16], U16, name="offs_sb")
+        two_sb = lists.tile([P, S // 16], U16, name="two_sb")
+        n1_sb = lists.tile([P, MEMBERS * S // 16], U16, name="n1_sb")
+        n2_sb = lists.tile([P, S // 16], U16, name="n2_sb")
+        n3_sb = lists.tile([P, S // 16], U16, name="n3_sb")
+
+        table_words = keep.tile([P, T], U32, name="table_words")
+        table_scales = keep.tile([P, T], U8, name="table_scales")
+        nc.vector.memset(table_scales[:].bitcast(I32), 0)
+        def load_columns(w, name, c0, c1):
+            raw = keep.tile([P, PACK, c1 - c0], F32, name=f"{name}_raw{c0}", tag="raw", bufs=2)
+            nc.sync.dma_start(raw[:], w.rearrange("(p j) c -> p j c", j=PACK)[:, :, c0:c1])
+            return raw
+
+        for q in range(4):
+            nc.scalar.dma_start(
+                table_scales[32 * q : 32 * q + 4, :].bitcast(I32), x_scales[0, 4 * q : 4 * q + 4, :].bitcast(I32)
+            )
+        gn_sb = keep.tile([P, PACK], F32, name="gn_sb")
+        nc.sync.dma_start(offs_sb[:], offs)
+        nc.sync.dma_start(two_sb[:], two)
+        nc.sync.dma_start(n1_sb[:], n1)
+        nc.sync.dma_start(n2_sb[:], n2)
+        nc.sync.dma_start(gn_sb[:], gn.rearrange("(p t) o -> p (t o)", t=PACK))
+        w1_first = load_columns(w1, "w1", 0, W1_SPLIT)
+        nc.sync.dma_start(table_words[:].bitcast(I32), x_words[0].rearrange("p n t -> p (n t)").bitcast(I32))
+        w1_last = load_columns(w1, "w1", W1_SPLIT, H)
+        nc.sync.dma_start(n3_sb[:], n3)
+
+        ex = [keep.tile([P, S + SPARE], F32, name=f"ex{t}") for t in range(PACK)]
+        for t in range(PACK):
+            nc.vector.memset(ex[t][:, S:], 0.0)
+
+        x1_words = keep.tile([P, S], U32, name="x1_words", align_bytes=64)
+        x1_scales = keep.tile([P, S], U8, name="x1_scales", align_bytes=64)
+        x2_scales = keep.tile([P, S], U8, name="x2_scales", align_bytes=64)
+        gather("vector", x1_scales[:], table_scales[:], offs_sb[:])
+        gather("vector", x2_scales[:], table_scales[:], two_sb[:])
+        gather("vector", x1_words[:], table_words[:], offs_sb[:])
+
+        def mx_tiles(name):
+            grouped = keep.tile([P, PACK * S], BF16, name=name + "_bf16", tag=name + "_bf16", align_bytes=64)
+            words = keep.tile([P, S], U32, name=name + "_words", align_bytes=64)
+            scales = keep.tile([P, S], U8, name=name + "_scales", align_bytes=64)
+            return grouped, words, scales
+
+        def quantise(tiles, c0, c1):
+            grouped, words, scales = tiles
+            nc.vector.quantize_mx(
+                out=words[:, c0:c1].bitcast(FP8X4), scales=scales[:, c0:c1], in_=grouped[:, PACK * c0 : PACK * c1]
+            )
+
+        w1_mx, w2_mx, w3_mx = mx_tiles("w1"), mx_tiles("w2"), mx_tiles("w3")
+        weave("scalar", w1_mx[0], w1_first, 0, W1_SPLIT // PACK, 0)
+        weave("scalar", w1_mx[0], w1_last, W1_SPLIT // PACK, P, W1_SPLIT // PACK)
+
+        for t in range(PACK):
+            quantise(w1_mx, t * P, (t + 1) * P)
+        for t in range(PACK):
+            cols = slice(t * P, (t + 1) * P)
+            y = psum.tile([P, S], F32, name=f"y{t}")
+            nc.tensor.matmul_mx(
+                out=y[:],
+                lhsT=w1_mx[1][:, cols].bitcast(FP8X4),
+                lhsT_scale=w1_mx[2][:, cols],
+                rhs=x1_words[:].bitcast(FP8X4),
+                rhs_scale=x1_scales[:],
+                start=True,
+                stop=True,
+            )
+            nc.scalar.activation(ex[t][:, :S], y[:], ACT.Exp, scale=0.5)
+
+        x2_words = keep.tile([P, S], U32, name="x2_words", tag="w1_bf16", align_bytes=64)
+        gather("vector", x2_words[:], table_words[:], two_sb[:])
+
+        h_bank = [psum.tile([P, PACK, CHUNK], F32, name=f"h{c}") for c in range(CHUNKS)]
+        h_sb = [keep.tile([P, S], F32, name=f"h_sb{t}") for t in range(PACK)]
+        members = [None] * CHUNKS
+        z_mx = [None] * CHUNKS
+
+        def look_up(c):
+            width = MEMBERS * CHUNK // 16
+            members[c] = keep.tile([P, PACK, MEMBERS * CHUNK], F32, name=f"members{c}", tag="members", bufs=2)
+            for t in range(PACK):
+                engine = "vector" if t == 0 or (c == 0 and t == 1) else "scalar"
+                gather(engine, members[c][:, t, :], ex[t][:], n1_sb[:, c * width : (c + 1) * width])
+
+        def normalise(c, groups):
+            cols = slice(c * CHUNK, (c + 1) * CHUNK)
+            pairs = keep.tile([P, PACK, CHUNK, 2], F32, name=f"pairs{c}")
+            denom = keep.tile([P, PACK, CHUNK], F32, name=f"denom{c}")
+            root = keep.tile([P, PACK, CHUNK], F32, name=f"root{c}")
+            recip = keep.tile([P, PACK, CHUNK], F32, name=f"recip{c}")
+            z_rows = keep.tile([P, PACK, CHUNK], BF16, name=f"z_rows{c}")
+            for t0, t1 in groups:
+                m = members[c][:, t0:t1, :].rearrange("p t (j u) -> p (t j) u", u=MEMBERS)
+                pr = pairs[:, t0:t1].rearrange("p t j u -> p (t j) u")
+                nc.vector.tensor_tensor(pr, m[:, :, 0:2], m[:, :, 2:4], ALU.add)
+                dn = denom[:, t0:t1].rearrange("p t j -> p (t j)")
+                nc.vector.scalar_tensor_tensor(dn, pr[:, :, 0], 0.5, pr[:, :, 1], ALU.add, ALU.add)
+                rt = root[:, t0:t1].rearrange("p t j -> p (t j)")
+                nc.scalar.activation(rt, dn, ACT.Abs_reciprocal_sqrt, scale=0.25)
+                rc = recip[:, t0:t1].rearrange("p t j -> p (t j)")
+                nc.scalar.activation(rc, rt, ACT.Square)
+                for t in range(t0, t1):
+                    nc.vector.scalar_tensor_tensor(
+                        z_rows[:, t, :], ex[t][:, cols], gn_sb[:, t : t + 1], recip[:, t, :], ALU.mult, ALU.mult
+                    )
+            grouped = keep.tile([P, PACK * CHUNK], BF16, name=f"z_bf16{c}", align_bytes=64)
+            words = keep.tile([P, CHUNK], U32, name=f"z_words{c}", align_bytes=64)
+            scales = keep.tile([P, CHUNK], U8, name=f"z_scales{c}", align_bytes=64)
+            nc.vector.tensor_copy(
+                grouped[:].rearrange("p (j t) -> p j t", t=PACK), z_rows[:].rearrange("p t j -> p j t")
+            )
+            z_mx[c] = (grouped, words, scales)
+            quantise(z_mx[c], 0, CHUNK)
+
+        def second_layer(c):
+            cols = slice(c * CHUNK, (c + 1) * CHUNK)
+            for t in range(PACK):
+                rows = slice(t * P, (t + 1) * P)
+                nc.tensor.matmul_mx(
+                    out=h_bank[c][:, t, :],
+                    lhsT=w3_mx[1][:, rows].bitcast(FP8X4),
+                    lhsT_scale=w3_mx[2][:, rows],
+                    rhs=x2_words[:, cols].bitcast(FP8X4),
+                    rhs_scale=x2_scales[:, cols],
+                    start=(t == 0),
+                    stop=False,
+                )
+            for t in range(PACK):
+                rows = slice(t * P, (t + 1) * P)
+                nc.tensor.matmul_mx(
+                    out=h_bank[c][:, t, :],
+                    lhsT=w2_mx[1][:, rows].bitcast(FP8X4),
+                    lhsT_scale=w2_mx[2][:, rows],
+                    rhs=z_mx[c][1][:].bitcast(FP8X4),
+                    rhs_scale=z_mx[c][2][:],
+                    start=False,
+                    stop=(t == PACK - 1),
+                )
+            for t in range(PACK):
+                nc.scalar.activation(h_sb[t][:, cols], h_bank[c][:, t, :], ACT.Copy)
+
+        whole = [(0, PACK)]
+        single = [(t, t + 1) for t in range(PACK)]
+        look_up(0)
+        for half in range(2):
+            weave("vector", w3_mx[0], load_columns(w3, "w3", HALF * half, HALF * half + HALF), 64 * half, 64 * half + 64, 64 * half)
+        look_up(1)
+        quantise(w3_mx, 0, S)
+        normalise(0, whole)
+        for half in range(2):
+            weave("vector", w2_mx[0], load_columns(w2, "w2", HALF * half, HALF * half + HALF), 64 * half, 64 * half + 64, 64 * half)
+        look_up(2)
+        quantise(w2_mx, 0, S)
+        normalise(1, whole)
+        second_layer(0)
+        look_up(3)
+        normalise(2, whole)
+        second_layer(1)
+        normalise(3, single)
+        second_layer(2)
+        second_layer(3)
+
+        out_rows = out.rearrange("(p t) n -> p t n", t=PACK)
+        for t in range(PACK):
+            at2 = keep.tile([P, S], F32, name=f"at2_{t}")
+            at3 = keep.tile([P, S], F32, name=f"at3_{t}")
+            down = keep.tile([P, S], F32, name=f"down{t}")
+            up = keep.tile([P, S], F32, name=f"up{t}")
+            up_half = keep.tile([P, S], F32, name=f"up_half{t}")
+            result = keep.tile([P, S], F32, name=f"result{t}")
+            for u in range(2):
+                cols = slice(u * HALF, (u + 1) * HALF)
+                entries = slice(u * HALF // 16, (u + 1) * HALF // 16)
+                gather("vector" if t == 0 else "scalar", at3[:, cols], h_sb[t][:], n3_sb[:, entries])
+                gather("scalar", at2[:, cols], h_sb[t][:], n2_sb[:, entries])
+            spans = [slice(0, S)] if t < PACK - 1 else [slice(0, HALF), slice(HALF, S)]
+            for cols in spans:
+                nc.vector.tensor_tensor(up[:, cols], at3[:, cols], h_sb[t][:, cols], ALU.subtract)
+                nc.vector.tensor_tensor(down[:, cols], h_sb[t][:, cols], at2[:, cols], ALU.subtract)
+                nc.vector.tensor_scalar(up_half[:, cols], up[:, cols], 0.0, 0.5, ALU.max, ALU.mult)
+                nc.vector.scalar_tensor_tensor(result[:, cols], down[:, cols], 0.0, up_half[:, cols], ALU.max, ALU.add)
+                nc.sync.dma_start(out_rows[:, t, cols], result[:, cols])

@@ -1,6 +1,7 @@
 from contextlib import ExitStack
 
 import concourse.mybir as mybir
+from concourse.masks import make_identity
 
 F32 = mybir.dt.float32
 BF16 = mybir.dt.bfloat16
@@ -20,7 +21,7 @@ CHUNK = 128
 CHUNKS = S // CHUNK
 SPARE = 32
 HALF = S // 2
-W1_SPLIT = 384
+W1_SPLIT = 84
 FLOPS = 3 * 2 * 512 * 512 * 512
 
 
@@ -56,35 +57,42 @@ def tile_picked_mixingsharehinge_none_p_kernel(tc, x_words, x_scales, w1, gn, w2
         table_scales = keep.tile([P, T], U8, name="table_scales")
         nc.vector.memset(table_scales[:].bitcast(I32), 0)
         def load_columns(w, name, c0, c1):
-            raw = keep.tile([P, PACK, c1 - c0], F32, name=f"{name}_raw{c0}", tag="raw", bufs=2)
+            raw = keep.tile([P, PACK, c1 - c0], F32, name=f"{name}_raw{c0}")
             nc.sync.dma_start(raw[:], w.rearrange("(p j) c -> p j c", j=PACK)[:, :, c0:c1])
             return raw
 
         for q in range(4):
-            nc.scalar.dma_start(
+            queue = nc.sync if q < 2 else nc.scalar
+            queue.dma_start(
                 table_scales[32 * q : 32 * q + 4, :].bitcast(I32), x_scales[0, 4 * q : 4 * q + 4, :].bitcast(I32)
             )
-        gn_sb = keep.tile([P, PACK], F32, name="gn_sb")
         nc.sync.dma_start(offs_sb[:], offs)
         nc.sync.dma_start(two_sb[:], two)
         nc.sync.dma_start(n1_sb[:], n1)
-        nc.sync.dma_start(n2_sb[:], n2)
-        nc.sync.dma_start(gn_sb[:], gn.rearrange("(p t) o -> p (t o)", t=PACK))
-        w1_first = load_columns(w1, "w1", 0, W1_SPLIT)
         nc.sync.dma_start(table_words[:].bitcast(I32), x_words[0].rearrange("p n t -> p (n t)").bitcast(I32))
-        w1_last = load_columns(w1, "w1", W1_SPLIT, H)
+        w1_raw = [load_columns(w1, "w1", 0, HALF), load_columns(w1, "w1", HALF, H)]
+        gn_sb = keep.tile([P, PACK], F32, name="gn_sb")
+        nc.sync.dma_start(gn_sb[:], gn.rearrange("(p t) o -> p (t o)", t=PACK))
+        w3_raw = load_columns(w3, "w3", 0, N)
+        w2_raw = load_columns(w2, "w2", 0, N)
+        nc.sync.dma_start(n2_sb[:], n2)
         nc.sync.dma_start(n3_sb[:], n3)
 
         ex = [keep.tile([P, S + SPARE], F32, name=f"ex{t}") for t in range(PACK)]
         for t in range(PACK):
             nc.vector.memset(ex[t][:, S:], 0.0)
 
+        identity = keep.tile([P, P], F32, name="identity")
+        make_identity(nc, identity[:])
+
         x1_words = keep.tile([P, S], U32, name="x1_words", align_bytes=64)
         x1_scales = keep.tile([P, S], U8, name="x1_scales", align_bytes=64)
+        x2_words = keep.tile([P, S], U32, name="x2_words", align_bytes=64)
         x2_scales = keep.tile([P, S], U8, name="x2_scales", align_bytes=64)
         gather("vector", x1_scales[:], table_scales[:], offs_sb[:])
         gather("vector", x2_scales[:], table_scales[:], two_sb[:])
         gather("vector", x1_words[:], table_words[:], offs_sb[:])
+        gather("vector", x2_words[:], table_words[:], two_sb[:])
 
         def mx_tiles(name):
             grouped = keep.tile([P, PACK * S], BF16, name=name + "_bf16", tag=name + "_bf16", align_bytes=64)
@@ -99,14 +107,15 @@ def tile_picked_mixingsharehinge_none_p_kernel(tc, x_words, x_scales, w1, gn, w2
             )
 
         w1_mx, w2_mx, w3_mx = mx_tiles("w1"), mx_tiles("w2"), mx_tiles("w3")
-        weave("scalar", w1_mx[0], w1_first, 0, W1_SPLIT // PACK, 0)
-        weave("scalar", w1_mx[0], w1_last, W1_SPLIT // PACK, P, W1_SPLIT // PACK)
+        weave("scalar", w1_mx[0], w1_raw[0], 0, 64, 0)
+        weave("scalar", w1_mx[0], w1_raw[1], 64, W1_SPLIT, 64)
+        weave("vector", w1_mx[0], w1_raw[1], W1_SPLIT, P, 64)
 
         for t in range(PACK):
             quantise(w1_mx, t * P, (t + 1) * P)
         for t in range(PACK):
             cols = slice(t * P, (t + 1) * P)
-            y = psum.tile([P, S], F32, name=f"y{t}")
+            y = psum.tile([P, S], F32, name=f"y{t}", tag=f"bank{t}")
             nc.tensor.matmul_mx(
                 out=y[:],
                 lhsT=w1_mx[1][:, cols].bitcast(FP8X4),
@@ -118,42 +127,58 @@ def tile_picked_mixingsharehinge_none_p_kernel(tc, x_words, x_scales, w1, gn, w2
             )
             nc.scalar.activation(ex[t][:, :S], y[:], ACT.Exp, scale=0.5)
 
-        x2_words = keep.tile([P, S], U32, name="x2_words", tag="w1_bf16", align_bytes=64)
-        gather("vector", x2_words[:], table_words[:], two_sb[:])
-
-        h_bank = [psum.tile([P, PACK, CHUNK], F32, name=f"h{c}") for c in range(CHUNKS)]
-        h_sb = [keep.tile([P, S], F32, name=f"h_sb{t}") for t in range(PACK)]
+        h_sb = [keep.tile([P, 2 * S], F32, name=f"h_sb{t}") for t in range(PACK)]
+        for t in range(PACK):
+            nc.vector.memset(h_sb[t][:, S:], 0.0)
         members = [None] * CHUNKS
         z_mx = [None] * CHUNKS
 
         def look_up(c):
             width = MEMBERS * CHUNK // 16
-            members[c] = keep.tile([P, PACK, MEMBERS * CHUNK], F32, name=f"members{c}", tag="members", bufs=2)
+            members[c] = keep.tile([P, PACK, MEMBERS * CHUNK], F32, name=f"members{c}", tag="members", bufs=4)
             for t in range(PACK):
-                engine = "vector" if t == 0 or (c == 0 and t == 1) else "scalar"
+                engine = "vector" if t < 2 else "scalar"
                 gather(engine, members[c][:, t, :], ex[t][:], n1_sb[:, c * width : (c + 1) * width])
 
-        def normalise(c, groups):
-            cols = slice(c * CHUNK, (c + 1) * CHUNK)
+        def recip_by_tensor(c):
+            sums = psum.tile([P, PACK, P], F32, name=f"sums{c}", tag=f"bank{c}")
+            for t in range(PACK):
+                planes = members[c][:, t, :].rearrange("p (j u) -> p u j", u=MEMBERS)
+                for u in range(MEMBERS):
+                    nc.tensor.matmul(
+                        sums[:, t, :], planes[:, u, :], identity[:],
+                        start=(u == 0), stop=(u == MEMBERS - 1), is_transpose=True,
+                    )
+            root = keep.tile([P, PACK, P], F32, name=f"root{c}")
+            square = keep.tile([P, PACK, P], F32, name=f"square{c}")
+            nc.scalar.activation(root[:], sums[:], ACT.Abs_reciprocal_sqrt, bias=0.125, scale=0.25)
+            nc.scalar.activation(square[:], root[:], ACT.Square)
+            recip = psum.tile([P, PACK, CHUNK], F32, name=f"recip{c}", tag=f"bank{c}")
+            for t in range(PACK):
+                nc.tensor.transpose(recip[:, t, :], square[:, t, :], identity[:])
+            return recip
+
+        def recip_by_vector(c):
             pairs = keep.tile([P, PACK, CHUNK, 2], F32, name=f"pairs{c}")
             denom = keep.tile([P, PACK, CHUNK], F32, name=f"denom{c}")
             root = keep.tile([P, PACK, CHUNK], F32, name=f"root{c}")
             recip = keep.tile([P, PACK, CHUNK], F32, name=f"recip{c}")
+            for t in range(PACK):
+                m = members[c][:, t, :].rearrange("p (j u) -> p j u", u=MEMBERS)
+                nc.vector.tensor_tensor(pairs[:, t], m[:, :, 0:2], m[:, :, 2:4], ALU.add)
+                nc.vector.tensor_tensor(denom[:, t], pairs[:, t, :, 0], pairs[:, t, :, 1], ALU.add)
+                nc.scalar.activation(root[:, t], denom[:, t], ACT.Abs_reciprocal_sqrt, bias=0.125, scale=0.25)
+                nc.scalar.activation(recip[:, t], root[:, t], ACT.Square)
+            return recip
+
+        def normalise(c):
+            cols = slice(c * CHUNK, (c + 1) * CHUNK)
+            recip = recip_by_vector(c) if c >= 3 else recip_by_tensor(c)
             z_rows = keep.tile([P, PACK, CHUNK], BF16, name=f"z_rows{c}")
-            for t0, t1 in groups:
-                m = members[c][:, t0:t1, :].rearrange("p t (j u) -> p (t j) u", u=MEMBERS)
-                pr = pairs[:, t0:t1].rearrange("p t j u -> p (t j) u")
-                nc.vector.tensor_tensor(pr, m[:, :, 0:2], m[:, :, 2:4], ALU.add)
-                dn = denom[:, t0:t1].rearrange("p t j -> p (t j)")
-                nc.vector.scalar_tensor_tensor(dn, pr[:, :, 0], 0.5, pr[:, :, 1], ALU.add, ALU.add)
-                rt = root[:, t0:t1].rearrange("p t j -> p (t j)")
-                nc.scalar.activation(rt, dn, ACT.Abs_reciprocal_sqrt, scale=0.25)
-                rc = recip[:, t0:t1].rearrange("p t j -> p (t j)")
-                nc.scalar.activation(rc, rt, ACT.Square)
-                for t in range(t0, t1):
-                    nc.vector.scalar_tensor_tensor(
-                        z_rows[:, t, :], ex[t][:, cols], gn_sb[:, t : t + 1], recip[:, t, :], ALU.mult, ALU.mult
-                    )
+            for t in range(PACK):
+                nc.vector.scalar_tensor_tensor(
+                    z_rows[:, t, :], ex[t][:, cols], gn_sb[:, t : t + 1], recip[:, t, :], ALU.mult, ALU.mult
+                )
             grouped = keep.tile([P, PACK * CHUNK], BF16, name=f"z_bf16{c}", align_bytes=64)
             words = keep.tile([P, CHUNK], U32, name=f"z_words{c}", align_bytes=64)
             scales = keep.tile([P, CHUNK], U8, name=f"z_scales{c}", align_bytes=64)
@@ -165,10 +190,11 @@ def tile_picked_mixingsharehinge_none_p_kernel(tc, x_words, x_scales, w1, gn, w2
 
         def second_layer(c):
             cols = slice(c * CHUNK, (c + 1) * CHUNK)
+            h_bank = psum.tile([P, PACK, CHUNK], F32, name=f"h{c}", tag=f"bank{c}")
             for t in range(PACK):
                 rows = slice(t * P, (t + 1) * P)
                 nc.tensor.matmul_mx(
-                    out=h_bank[c][:, t, :],
+                    out=h_bank[:, t, :],
                     lhsT=w3_mx[1][:, rows].bitcast(FP8X4),
                     lhsT_scale=w3_mx[2][:, rows],
                     rhs=x2_words[:, cols].bitcast(FP8X4),
@@ -179,7 +205,7 @@ def tile_picked_mixingsharehinge_none_p_kernel(tc, x_words, x_scales, w1, gn, w2
             for t in range(PACK):
                 rows = slice(t * P, (t + 1) * P)
                 nc.tensor.matmul_mx(
-                    out=h_bank[c][:, t, :],
+                    out=h_bank[:, t, :],
                     lhsT=w2_mx[1][:, rows].bitcast(FP8X4),
                     lhsT_scale=w2_mx[2][:, rows],
                     rhs=z_mx[c][1][:].bitcast(FP8X4),
@@ -188,28 +214,22 @@ def tile_picked_mixingsharehinge_none_p_kernel(tc, x_words, x_scales, w1, gn, w2
                     stop=(t == PACK - 1),
                 )
             for t in range(PACK):
-                nc.scalar.activation(h_sb[t][:, cols], h_bank[c][:, t, :], ACT.Copy)
+                nc.scalar.activation(h_sb[t][:, cols], h_bank[:, t, :], ACT.Copy)
 
-        whole = [(0, PACK)]
-        single = [(t, t + 1) for t in range(PACK)]
+        def prepare(w_mx, w_raw):
+            for part in range(2):
+                weave("vector", w_mx[0], w_raw, 64 * part, 64 * (part + 1), 0)
+            quantise(w_mx, 0, S)
+
         look_up(0)
-        for half in range(2):
-            weave("vector", w3_mx[0], load_columns(w3, "w3", HALF * half, HALF * half + HALF), 64 * half, 64 * half + 64, 64 * half)
-        look_up(1)
-        quantise(w3_mx, 0, S)
-        normalise(0, whole)
-        for half in range(2):
-            weave("vector", w2_mx[0], load_columns(w2, "w2", HALF * half, HALF * half + HALF), 64 * half, 64 * half + 64, 64 * half)
-        look_up(2)
-        quantise(w2_mx, 0, S)
-        normalise(1, whole)
-        second_layer(0)
-        look_up(3)
-        normalise(2, whole)
-        second_layer(1)
-        normalise(3, single)
-        second_layer(2)
-        second_layer(3)
+        for c in range(1, CHUNKS):
+            look_up(c)
+            normalise(c - 1)
+        prepare(w3_mx, w3_raw)
+        prepare(w2_mx, w2_raw)
+        normalise(CHUNKS - 1)
+        for c in range(CHUNKS):
+            second_layer(c)
 
         out_rows = out.rearrange("(p t) n -> p t n", t=PACK)
         for t in range(PACK):
@@ -219,12 +239,13 @@ def tile_picked_mixingsharehinge_none_p_kernel(tc, x_words, x_scales, w1, gn, w2
             up = keep.tile([P, S], F32, name=f"up{t}")
             up_half = keep.tile([P, S], F32, name=f"up_half{t}")
             result = keep.tile([P, S], F32, name=f"result{t}")
-            for u in range(2):
-                cols = slice(u * HALF, (u + 1) * HALF)
-                entries = slice(u * HALF // 16, (u + 1) * HALF // 16)
-                gather("vector" if t == 0 else "scalar", at3[:, cols], h_sb[t][:], n3_sb[:, entries])
-                gather("scalar", at2[:, cols], h_sb[t][:], n2_sb[:, entries])
             spans = [slice(0, S)] if t < PACK - 1 else [slice(0, HALF), slice(HALF, S)]
+            for cols in spans:
+                entries = slice(cols.start // 16, cols.stop // 16)
+                gather("vector" if t == 0 else "scalar", at3[:, cols], h_sb[t][:], n3_sb[:, entries])
+            for cols in spans:
+                entries = slice(cols.start // 16, cols.stop // 16)
+                gather("scalar", at2[:, cols], h_sb[t][:], n2_sb[:, entries])
             for cols in spans:
                 nc.vector.tensor_tensor(up[:, cols], at3[:, cols], h_sb[t][:, cols], ALU.subtract)
                 nc.vector.tensor_tensor(down[:, cols], h_sb[t][:, cols], at2[:, cols], ALU.subtract)

@@ -39,6 +39,8 @@ def tile_picked_mixingsharehinge_none_p_kernel(tc, x_words, x_scales, w1, gn, w2
         src = raw[:].rearrange("p j (m t) -> p m t j", t=PACK)[:, m0 - raw_m0 : m1 - raw_m0]
         if engine == "vector":
             nc.vector.tensor_copy(dst, src)
+        elif engine == "gpsimd":
+            nc.gpsimd.tensor_scalar(dst, src, 1.0, 0.0, ALU.mult, ALU.add)
         else:
             nc.scalar.activation(dst, src, ACT.Copy)
 
@@ -87,12 +89,10 @@ def tile_picked_mixingsharehinge_none_p_kernel(tc, x_words, x_scales, w1, gn, w2
 
         x1_words = keep.tile([P, S], U32, name="x1_words", align_bytes=64)
         x1_scales = keep.tile([P, S], U8, name="x1_scales", align_bytes=64)
-        x2_words = keep.tile([P, S], U32, name="x2_words", align_bytes=64)
         x2_scales = keep.tile([P, S], U8, name="x2_scales", align_bytes=64)
         gather("vector", x1_scales[:], table_scales[:], offs_sb[:])
         gather("vector", x2_scales[:], table_scales[:], two_sb[:])
         gather("vector", x1_words[:], table_words[:], offs_sb[:])
-        gather("vector", x2_words[:], table_words[:], two_sb[:])
 
         def mx_tiles(name):
             grouped = keep.tile([P, PACK * S], BF16, name=name + "_bf16", tag=name + "_bf16", align_bytes=64)
@@ -127,6 +127,9 @@ def tile_picked_mixingsharehinge_none_p_kernel(tc, x_words, x_scales, w1, gn, w2
             )
             nc.scalar.activation(ex[t][:, :S], y[:], ACT.Exp, scale=0.5)
 
+        x2_words = keep.tile([P, S], U32, name="x2_words", tag="w1_bf16", align_bytes=64)
+        gather("vector", x2_words[:], table_words[:], two_sb[:])
+
         h_sb = [keep.tile([P, 2 * S], F32, name=f"h_sb{t}") for t in range(PACK)]
         for t in range(PACK):
             nc.vector.memset(h_sb[t][:, S:], 0.0)
@@ -137,7 +140,7 @@ def tile_picked_mixingsharehinge_none_p_kernel(tc, x_words, x_scales, w1, gn, w2
             width = MEMBERS * CHUNK // 16
             members[c] = keep.tile([P, PACK, MEMBERS * CHUNK], F32, name=f"members{c}", tag="members", bufs=4)
             for t in range(PACK):
-                engine = "vector" if t < 2 else "scalar"
+                engine = "vector" if t<2 else "scalar"
                 gather(engine, members[c][:, t, :], ex[t][:], n1_sb[:, c * width : (c + 1) * width])
 
         def recip_by_tensor(c):
@@ -163,17 +166,20 @@ def tile_picked_mixingsharehinge_none_p_kernel(tc, x_words, x_scales, w1, gn, w2
             denom = keep.tile([P, PACK, CHUNK], F32, name=f"denom{c}")
             root = keep.tile([P, PACK, CHUNK], F32, name=f"root{c}")
             recip = keep.tile([P, PACK, CHUNK], F32, name=f"recip{c}")
-            for t in range(PACK):
-                m = members[c][:, t, :].rearrange("p (j u) -> p j u", u=MEMBERS)
-                nc.vector.tensor_tensor(pairs[:, t], m[:, :, 0:2], m[:, :, 2:4], ALU.add)
-                nc.vector.tensor_tensor(denom[:, t], pairs[:, t, :, 0], pairs[:, t, :, 1], ALU.add)
-                nc.scalar.activation(root[:, t], denom[:, t], ACT.Abs_reciprocal_sqrt, bias=0.125, scale=0.25)
-                nc.scalar.activation(recip[:, t], root[:, t], ACT.Square)
+            step = 1 if c == CHUNKS - 1 else PACK
+            for t in range(0, PACK, step):
+                ts = slice(t, t + step)
+                m = members[c][:, ts, :].rearrange("p t (j u) -> p (t j) u", u=MEMBERS)
+                two_sums = pairs[:, ts].rearrange("p t j u -> p (t j) u")
+                nc.vector.tensor_tensor(two_sums, m[:, :, 0:2], m[:, :, 2:4], ALU.add)
+                nc.vector.tensor_tensor(denom[:, ts], pairs[:, ts, :, 0], pairs[:, ts, :, 1], ALU.add)
+                nc.scalar.activation(root[:, ts], denom[:, ts], ACT.Abs_reciprocal_sqrt, bias=0.125, scale=0.25)
+                nc.scalar.activation(recip[:, ts], root[:, ts], ACT.Square)
             return recip
 
         def normalise(c):
             cols = slice(c * CHUNK, (c + 1) * CHUNK)
-            recip = recip_by_vector(c) if c >= 3 else recip_by_tensor(c)
+            recip = recip_by_vector(c) if c >= 2 else recip_by_tensor(c)
             z_rows = keep.tile([P, PACK, CHUNK], BF16, name=f"z_rows{c}")
             for t in range(PACK):
                 nc.vector.scalar_tensor_tensor(
@@ -188,51 +194,55 @@ def tile_picked_mixingsharehinge_none_p_kernel(tc, x_words, x_scales, w1, gn, w2
             z_mx[c] = (grouped, words, scales)
             quantise(z_mx[c], 0, CHUNK)
 
+        def product(acc, w_mx, t, words, scales, start, stop):
+            rows = slice(t * P, (t + 1) * P)
+            nc.tensor.matmul_mx(
+                out=acc,
+                lhsT=w_mx[1][:, rows].bitcast(FP8X4),
+                lhsT_scale=w_mx[2][:, rows],
+                rhs=words.bitcast(FP8X4),
+                rhs_scale=scales,
+                start=start,
+                stop=stop,
+            )
+
         def second_layer(c):
             cols = slice(c * CHUNK, (c + 1) * CHUNK)
             h_bank = psum.tile([P, PACK, CHUNK], F32, name=f"h{c}", tag=f"bank{c}")
             for t in range(PACK):
-                rows = slice(t * P, (t + 1) * P)
-                nc.tensor.matmul_mx(
-                    out=h_bank[:, t, :],
-                    lhsT=w3_mx[1][:, rows].bitcast(FP8X4),
-                    lhsT_scale=w3_mx[2][:, rows],
-                    rhs=x2_words[:, cols].bitcast(FP8X4),
-                    rhs_scale=x2_scales[:, cols],
-                    start=(t == 0),
-                    stop=False,
-                )
+                product(h_bank[:, t, :], w3_mx, t, x2_words[:, cols], x2_scales[:, cols], t == 0, False)
             for t in range(PACK):
-                rows = slice(t * P, (t + 1) * P)
-                nc.tensor.matmul_mx(
-                    out=h_bank[:, t, :],
-                    lhsT=w2_mx[1][:, rows].bitcast(FP8X4),
-                    lhsT_scale=w2_mx[2][:, rows],
-                    rhs=z_mx[c][1][:].bitcast(FP8X4),
-                    rhs_scale=z_mx[c][2][:],
-                    start=False,
-                    stop=(t == PACK - 1),
-                )
+                product(h_bank[:, t, :], w2_mx, t, z_mx[c][1][:], z_mx[c][2][:], False, t == PACK - 1)
             for t in range(PACK):
                 nc.scalar.activation(h_sb[t][:, cols], h_bank[:, t, :], ACT.Copy)
 
         def prepare(w_mx, w_raw):
-            for part in range(2):
-                weave("vector", w_mx[0], w_raw, 64 * part, 64 * (part + 1), 0)
+            for part in range(4):
+                weave("gpsimd", w_mx[0], w_raw, 32 * part, 32 * (part + 1), 0)
             quantise(w_mx, 0, S)
 
         look_up(0)
-        for c in range(1, CHUNKS):
-            look_up(c)
-            normalise(c - 1)
+        look_up(1)
+        look_up(2)
+        look_up(3)
+        normalise(0)
+        normalise(1)
         prepare(w3_mx, w3_raw)
         prepare(w2_mx, w2_raw)
-        normalise(CHUNKS - 1)
-        for c in range(CHUNKS):
+        normalise(2)
+        normalise(3)
+        for c in range(CHUNKS - 1):
             second_layer(c)
+        last = slice(S - CHUNK, S)
+        h_last = [psum.tile([P, CHUNK], F32, name=f"h_last{t}") for t in range(PACK)]
+        for t in range(PACK):
+            product(h_last[t][:], w3_mx, t, x2_words[:, last], x2_scales[:, last], True, False)
+        for t in range(PACK):
+            product(h_last[t][:], w2_mx, t, z_mx[-1][1][:], z_mx[-1][2][:], False, True)
 
         out_rows = out.rearrange("(p t) n -> p t n", t=PACK)
         for t in range(PACK):
+            nc.scalar.activation(h_sb[t][:, last], h_last[t][:], ACT.Copy)
             at2 = keep.tile([P, S], F32, name=f"at2_{t}")
             at3 = keep.tile([P, S], F32, name=f"at3_{t}")
             down = keep.tile([P, S], F32, name=f"down{t}")

@@ -21,7 +21,7 @@ CHUNK = 128
 CHUNKS = S // CHUNK
 SPARE = 32
 HALF = S // 2
-W1_SPLIT = 84
+W1_PIECES = ((0, 256), (256, 384), (384, 512))
 FLOPS = 3 * 2 * 512 * 512 * 512
 
 
@@ -70,9 +70,9 @@ def tile_picked_mixingsharehinge_none_p_kernel(tc, x_words, x_scales, w1, gn, w2
             )
         nc.sync.dma_start(offs_sb[:], offs)
         nc.sync.dma_start(two_sb[:], two)
-        nc.sync.dma_start(n1_sb[:], n1)
         nc.sync.dma_start(table_words[:].bitcast(I32), x_words[0].rearrange("p n t -> p (n t)").bitcast(I32))
-        w1_raw = [load_columns(w1, "w1", 0, HALF), load_columns(w1, "w1", HALF, H)]
+        w1_raw = [load_columns(w1, "w1", c0, c1) for c0, c1 in W1_PIECES]
+        nc.sync.dma_start(n1_sb[:], n1)
         gn_sb = keep.tile([P, PACK], F32, name="gn_sb")
         nc.sync.dma_start(gn_sb[:], gn.rearrange("(p t) o -> p (t o)", t=PACK))
         w3_raw = load_columns(w3, "w3", 0, N)
@@ -94,10 +94,10 @@ def tile_picked_mixingsharehinge_none_p_kernel(tc, x_words, x_scales, w1, gn, w2
         gather("vector", x2_scales[:], table_scales[:], two_sb[:])
         gather("vector", x1_words[:], table_words[:], offs_sb[:])
 
-        def mx_tiles(name):
-            grouped = keep.tile([P, PACK * S], BF16, name=name + "_bf16", tag=name + "_bf16", align_bytes=64)
-            words = keep.tile([P, S], U32, name=name + "_words", align_bytes=64)
-            scales = keep.tile([P, S], U8, name=name + "_scales", align_bytes=64)
+        def mx_tiles(name, width):
+            grouped = keep.tile([P, PACK * width], BF16, name=name + "_bf16", tag=name + "_bf16", align_bytes=64)
+            words = keep.tile([P, width], U32, name=name + "_words", align_bytes=64)
+            scales = keep.tile([P, width], U8, name=name + "_scales", align_bytes=64)
             return grouped, words, scales
 
         def quantise(tiles, c0, c1):
@@ -106,10 +106,12 @@ def tile_picked_mixingsharehinge_none_p_kernel(tc, x_words, x_scales, w1, gn, w2
                 out=words[:, c0:c1].bitcast(FP8X4), scales=scales[:, c0:c1], in_=grouped[:, PACK * c0 : PACK * c1]
             )
 
-        w1_mx, w2_mx, w3_mx = mx_tiles("w1"), mx_tiles("w2"), mx_tiles("w3")
-        weave("scalar", w1_mx[0], w1_raw[0], 0, 64, 0)
-        weave("scalar", w1_mx[0], w1_raw[1], 64, W1_SPLIT, 64)
-        weave("vector", w1_mx[0], w1_raw[1], W1_SPLIT, P, 64)
+        w1_mx, w2_mx, w3_mx = mx_tiles("w1", H), mx_tiles("w2", N), mx_tiles("w3", N)
+        weave("scalar", w1_mx[0], w1_raw[0], 0, 40, 0)
+        weave("vector", w1_mx[0], w1_raw[0], 40, 64, 0)
+        weave("vector", w1_mx[0], w1_raw[1], 64, 96, 64)
+        weave("scalar", w1_mx[0], w1_raw[2], 96, 106, 96)
+        weave("vector", w1_mx[0], w1_raw[2], 106, P, 96)
 
         for t in range(PACK):
             quantise(w1_mx, t * P, (t + 1) * P)
@@ -130,69 +132,68 @@ def tile_picked_mixingsharehinge_none_p_kernel(tc, x_words, x_scales, w1, gn, w2
         x2_words = keep.tile([P, S], U32, name="x2_words", tag="w1_bf16", align_bytes=64)
         gather("vector", x2_words[:], table_words[:], two_sb[:])
 
-        h_sb = [keep.tile([P, 2 * S], F32, name=f"h_sb{t}") for t in range(PACK)]
-        for t in range(PACK):
+        h_sb = [keep.tile([P, S if t == PACK - 1 else 2 * S], F32, name=f"h_sb{t}") for t in range(PACK)]
+        for t in range(PACK - 1):
             nc.vector.memset(h_sb[t][:, S:], 0.0)
-        members = [None] * CHUNKS
-        z_mx = [None] * CHUNKS
+        front = [keep.tile([P, CHUNKS, MEMBERS * CHUNK], F32, name=f"front{t}") for t in range(2)]
+        back = [keep.tile([P, 2, MEMBERS * CHUNK], F32, name=f"back{c}") for c in range(CHUNKS)]
+        z_rows = keep.tile([P, PACK, S], BF16, name="z_rows")
 
-        def look_up(c):
+        def look_up(engine, t, c):
             width = MEMBERS * CHUNK // 16
-            members[c] = keep.tile([P, PACK, MEMBERS * CHUNK], F32, name=f"members{c}", tag="members", bufs=4)
-            for t in range(PACK):
-                engine = "vector" if t<2 else "scalar"
-                gather(engine, members[c][:, t, :], ex[t][:], n1_sb[:, c * width : (c + 1) * width])
+            dst = front[t][:, c, :] if t < 2 else back[c][:, t - 2, :]
+            gather(engine, dst, ex[t][:], n1_sb[:, c * width : (c + 1) * width])
 
-        def recip_by_tensor(c):
-            sums = psum.tile([P, PACK, P], F32, name=f"sums{c}", tag=f"bank{c}")
-            for t in range(PACK):
-                planes = members[c][:, t, :].rearrange("p (j u) -> p u j", u=MEMBERS)
+        def inverse(out_ap, root, sums):
+            nc.scalar.activation(root, sums, ACT.Abs_reciprocal_sqrt, bias=0.125, scale=0.25)
+            nc.scalar.activation(out_ap, root, ACT.Square)
+
+        def scale(t, cols, recip):
+            nc.vector.scalar_tensor_tensor(
+                z_rows[:, t, cols], ex[t][:, cols], gn_sb[:, t : t + 1], recip, ALU.mult, ALU.mult
+            )
+
+        def front_rows(t):
+            sums = psum.tile([P, CHUNKS, P], F32, name=f"sums{t}", tag=f"bank{t}")
+            for c in range(CHUNKS):
+                planes = front[t][:, c, :].rearrange("p (j u) -> p u j", u=MEMBERS)
                 for u in range(MEMBERS):
                     nc.tensor.matmul(
-                        sums[:, t, :], planes[:, u, :], identity[:],
+                        sums[:, c, :], planes[:, u, :], identity[:],
                         start=(u == 0), stop=(u == MEMBERS - 1), is_transpose=True,
                     )
-            root = keep.tile([P, PACK, P], F32, name=f"root{c}")
-            square = keep.tile([P, PACK, P], F32, name=f"square{c}")
-            nc.scalar.activation(root[:], sums[:], ACT.Abs_reciprocal_sqrt, bias=0.125, scale=0.25)
-            nc.scalar.activation(square[:], root[:], ACT.Square)
-            recip = psum.tile([P, PACK, CHUNK], F32, name=f"recip{c}", tag=f"bank{c}")
-            for t in range(PACK):
-                nc.tensor.transpose(recip[:, t, :], square[:, t, :], identity[:])
-            return recip
+            root = keep.tile([P, CHUNKS, P], F32, name=f"root{t}")
+            square = keep.tile([P, CHUNKS, P], F32, name=f"square{t}")
+            inverse(square[:], root[:], sums[:])
+            recip = psum.tile([P, S], F32, name=f"recip{t}", tag=f"bank{t}")
+            for c in range(CHUNKS):
+                nc.tensor.transpose(recip[:, c * CHUNK : (c + 1) * CHUNK], square[:, c, :], identity[:])
+            scale(t, slice(0, S), recip[:])
 
-        def recip_by_vector(c):
-            pairs = keep.tile([P, PACK, CHUNK, 2], F32, name=f"pairs{c}")
-            denom = keep.tile([P, PACK, CHUNK], F32, name=f"denom{c}")
-            root = keep.tile([P, PACK, CHUNK], F32, name=f"root{c}")
-            recip = keep.tile([P, PACK, CHUNK], F32, name=f"recip{c}")
-            step = 1 if c == CHUNKS - 1 else PACK
-            for t in range(0, PACK, step):
-                ts = slice(t, t + step)
-                m = members[c][:, ts, :].rearrange("p t (j u) -> p (t j) u", u=MEMBERS)
-                two_sums = pairs[:, ts].rearrange("p t j u -> p (t j) u")
-                nc.vector.tensor_tensor(two_sums, m[:, :, 0:2], m[:, :, 2:4], ALU.add)
-                nc.vector.tensor_tensor(denom[:, ts], pairs[:, ts, :, 0], pairs[:, ts, :, 1], ALU.add)
-                nc.scalar.activation(root[:, ts], denom[:, ts], ACT.Abs_reciprocal_sqrt, bias=0.125, scale=0.25)
-                nc.scalar.activation(recip[:, ts], root[:, ts], ACT.Square)
-            return recip
-
-        def normalise(c):
+        def back_rows(c, engine):
             cols = slice(c * CHUNK, (c + 1) * CHUNK)
-            recip = recip_by_vector(c) if c >= 2 else recip_by_tensor(c)
-            z_rows = keep.tile([P, PACK, CHUNK], BF16, name=f"z_rows{c}")
-            for t in range(PACK):
-                nc.vector.scalar_tensor_tensor(
-                    z_rows[:, t, :], ex[t][:, cols], gn_sb[:, t : t + 1], recip[:, t, :], ALU.mult, ALU.mult
-                )
-            grouped = keep.tile([P, PACK * CHUNK], BF16, name=f"z_bf16{c}", align_bytes=64)
-            words = keep.tile([P, CHUNK], U32, name=f"z_words{c}", align_bytes=64)
-            scales = keep.tile([P, CHUNK], U8, name=f"z_scales{c}", align_bytes=64)
-            nc.vector.tensor_copy(
-                grouped[:].rearrange("p (j t) -> p j t", t=PACK), z_rows[:].rearrange("p t j -> p j t")
-            )
-            z_mx[c] = (grouped, words, scales)
-            quantise(z_mx[c], 0, CHUNK)
+            pairs = keep.tile([P, 2 * CHUNK, 2], F32, name=f"pairs{c}")
+            sums = keep.tile([P, 2 * CHUNK], F32, name=f"sums_sb{c}")
+            root = keep.tile([P, 2 * CHUNK], F32, name=f"root_sb{c}")
+            recip = keep.tile([P, 2, CHUNK], F32, name=f"recip_sb{c}")
+            four = back[c][:].rearrange("p t (j u) -> p (t j) u", u=MEMBERS)
+            engine.tensor_tensor(pairs[:], four[:, :, 0:2], four[:, :, 2:4], ALU.add)
+            engine.tensor_tensor(sums[:], pairs[:, :, 0], pairs[:, :, 1], ALU.add)
+            inverse(recip[:].rearrange("p t j -> p (t j)"), root[:], sums[:])
+            for i in range(2):
+                scale(2 + i, cols, recip[:, i, :])
+
+        def quantise_z(cols):
+            width = cols.stop - cols.start
+            z_mx = mx_tiles(f"z{cols.start}", width)
+            dst = z_mx[0][:].rearrange("p (j t) -> p j t", t=PACK)
+            src = z_rows[:, :, cols].rearrange("p t j -> p j t")
+            if cols.start // CHUNK in (1,):
+                nc.scalar.copy(dst, src)
+            else:
+                nc.vector.tensor_copy(dst, src)
+            quantise(z_mx, 0, width)
+            return z_mx
 
         def product(acc, w_mx, t, words, scales, start, stop):
             rows = slice(t * P, (t + 1) * P)
@@ -206,59 +207,70 @@ def tile_picked_mixingsharehinge_none_p_kernel(tc, x_words, x_scales, w1, gn, w2
                 stop=stop,
             )
 
-        def second_layer(c):
-            cols = slice(c * CHUNK, (c + 1) * CHUNK)
-            h_bank = psum.tile([P, PACK, CHUNK], F32, name=f"h{c}", tag=f"bank{c}")
-            for t in range(PACK):
-                product(h_bank[:, t, :], w3_mx, t, x2_words[:, cols], x2_scales[:, cols], t == 0, False)
-            for t in range(PACK):
-                product(h_bank[:, t, :], w2_mx, t, z_mx[c][1][:], z_mx[c][2][:], False, t == PACK - 1)
-            for t in range(PACK):
-                nc.scalar.activation(h_sb[t][:, cols], h_bank[:, t, :], ACT.Copy)
+        def second_layer(cols, z_mx, tags):
+            width = cols.stop - cols.start
+            share = PACK // len(tags)
+            sums = []
+            for b, tag in enumerate(tags):
+                bank = psum.tile([P, share, width], F32, name=f"h{cols.start}_{b}", tag=tag)
+                for i in range(share):
+                    product(bank[:, i, :], w3_mx, b * share + i, x2_words[:, cols], x2_scales[:, cols], i == 0, False)
+                for i in range(share):
+                    product(bank[:, i, :], w2_mx, b * share + i, z_mx[1][:], z_mx[2][:], False, i == share - 1)
+                    sums.append(bank[:, i, :])
+            return sums
+
+        def copy_out(t, cols, sums):
+            if cols.start // CHUNK in (2,):
+                nc.vector.tensor_copy(h_sb[t][:, cols], sums[t])
+            else:
+                nc.scalar.activation(h_sb[t][:, cols], sums[t], ACT.Copy)
 
         def prepare(w_mx, w_raw):
             for part in range(4):
                 weave("gpsimd", w_mx[0], w_raw, 32 * part, 32 * (part + 1), 0)
             quantise(w_mx, 0, S)
 
-        look_up(0)
-        look_up(1)
-        look_up(2)
-        look_up(3)
-        normalise(0)
-        normalise(1)
+        last = slice(S - CHUNK, S)
+        for t in range(2):
+            for c in range(CHUNKS):
+                look_up("vector", t, c)
+        for c in range(CHUNKS):
+            for t in (2, 3):
+                look_up("vector" if (c, t) == (3, 2) else "scalar", t, c)
         prepare(w3_mx, w3_raw)
         prepare(w2_mx, w2_raw)
-        normalise(2)
-        normalise(3)
+        for t in range(2):
+            front_rows(t)
+        h_psum = []
+        for c in range(CHUNKS):
+            cols = slice(c * CHUNK, (c + 1) * CHUNK)
+            back_rows(c, nc.gpsimd if c < 2 else nc.vector)
+            tags = (f"bank{c}",) if c < CHUNKS - 1 else ("bank4", "bank5", "bank6", "bank7")
+            h_psum.append(second_layer(cols, quantise_z(cols), tags))
         for c in range(CHUNKS - 1):
-            second_layer(c)
-        last = slice(S - CHUNK, S)
-        h_last = [psum.tile([P, CHUNK], F32, name=f"h_last{t}") for t in range(PACK)]
-        for t in range(PACK):
-            product(h_last[t][:], w3_mx, t, x2_words[:, last], x2_scales[:, last], True, False)
-        for t in range(PACK):
-            product(h_last[t][:], w2_mx, t, z_mx[-1][1][:], z_mx[-1][2][:], False, True)
+            for t in range(PACK):
+                copy_out(t, slice(c * CHUNK, (c + 1) * CHUNK), h_psum[c])
+        h_last = h_psum[-1]
 
         out_rows = out.rearrange("(p t) n -> p t n", t=PACK)
         for t in range(PACK):
-            nc.scalar.activation(h_sb[t][:, last], h_last[t][:], ACT.Copy)
+            copy_out(t, last, h_last)
             at2 = keep.tile([P, S], F32, name=f"at2_{t}")
             at3 = keep.tile([P, S], F32, name=f"at3_{t}")
             down = keep.tile([P, S], F32, name=f"down{t}")
             up = keep.tile([P, S], F32, name=f"up{t}")
             up_half = keep.tile([P, S], F32, name=f"up_half{t}")
             result = keep.tile([P, S], F32, name=f"result{t}")
-            spans = [slice(0, S)] if t < PACK - 1 else [slice(0, HALF), slice(HALF, S)]
-            for cols in spans:
-                entries = slice(cols.start // 16, cols.stop // 16)
-                gather("vector" if t == 0 else "scalar", at3[:, cols], h_sb[t][:], n3_sb[:, entries])
-            for cols in spans:
-                entries = slice(cols.start // 16, cols.stop // 16)
-                gather("scalar", at2[:, cols], h_sb[t][:], n2_sb[:, entries])
-            for cols in spans:
-                nc.vector.tensor_tensor(up[:, cols], at3[:, cols], h_sb[t][:, cols], ALU.subtract)
-                nc.vector.tensor_tensor(down[:, cols], h_sb[t][:, cols], at2[:, cols], ALU.subtract)
+            h = h_sb[t][:, :S]
+            halves = [slice(0, S)] if t < PACK - 1 else [slice(0, HALF), slice(HALF, S)]
+            for cols in halves:
+                gather("vector" if t == 0 else "scalar", at3[:, cols], h_sb[t][:], n3_sb[:, cols.start // 16 : cols.stop // 16])
+                nc.vector.tensor_tensor(up[:, cols], at3[:, cols], h[:, cols], ALU.subtract)
                 nc.vector.tensor_scalar(up_half[:, cols], up[:, cols], 0.0, 0.5, ALU.max, ALU.mult)
+            spans = [slice(0, S)] if t < PACK - 1 else halves
+            for cols in spans:
+                gather("scalar", at2[:, cols], h_sb[t][:], n2_sb[:, cols.start // 16 : cols.stop // 16])
+                nc.vector.tensor_tensor(down[:, cols], h[:, cols], at2[:, cols], ALU.subtract)
                 nc.vector.scalar_tensor_tensor(result[:, cols], down[:, cols], 0.0, up_half[:, cols], ALU.max, ALU.add)
                 nc.sync.dma_start(out_rows[:, t, cols], result[:, cols])

@@ -15,17 +15,26 @@ ACT = mybir.ActivationFunctionType
 
 P = 128
 PACK = 4
-K, T, S, H, N = 512, 2048, 512, 512, 512
+T, S, H, N = 2048, 512, 512, 512
 MEMBERS = 4
+LIST = 16
 CHUNK = 128
 CHUNKS = S // CHUNK
-SPARE = 32
 HALF = S // 2
+FRONT = 2
+EX_SPARE = 32
+
 W1_PIECES = ((0, 256), (256, 384), (384, 512))
+W1_CUT_FIRST, W1_CUT_LAST = 40, 106
+GPSIMD_PARTS = 4
+Z_CHUNK_ON_SCALAR, H_CHUNK_ON_VECTOR = 1, 2
+
 FLOPS = 3 * 2 * 512 * 512 * 512
 
 
-def tile_picked_mixingsharehinge_none_p_kernel(tc, x_words, x_scales, w1, gn, w2, w3, offs, n1, two, n2, n3, out):
+def tile_picked_mixingsharehinge_none_p_kernel(
+    tc, x_words, x_scales, w1, gn, w2, w3, offs, n1, two, n2, n3, out
+):
     nc = tc.nc
 
     def gather(engine, dst, window, offsets):
@@ -34,7 +43,7 @@ def tile_picked_mixingsharehinge_none_p_kernel(tc, x_words, x_scales, w1, gn, w2
         else:
             nc.scalar.activation(dst, window.indirect(offsets), ACT.Copy)
 
-    def weave(engine, grouped, raw, m0, m1, raw_m0):
+    def interleave_weight(engine, grouped, raw, m0, m1, raw_m0):
         dst = grouped[:].rearrange("p (t m j) -> p m t j", t=PACK, j=PACK)[:, m0:m1]
         src = raw[:].rearrange("p j (m t) -> p m t j", t=PACK)[:, m0 - raw_m0 : m1 - raw_m0]
         if engine == "vector":
@@ -44,25 +53,31 @@ def tile_picked_mixingsharehinge_none_p_kernel(tc, x_words, x_scales, w1, gn, w2
         else:
             nc.scalar.activation(dst, src, ACT.Copy)
 
+    def chunk_columns(c):
+        return slice(c * CHUNK, (c + 1) * CHUNK)
+
+    def list_columns(entries):
+        return slice(entries.start // LIST, entries.stop // LIST)
+
     with ExitStack() as ctx:
         lists = ctx.enter_context(tc.tile_pool(name="lists", bufs=1))
         keep = ctx.enter_context(tc.tile_pool(name="keep", bufs=1))
         psum = ctx.enter_context(tc.psum_pool(name="psum", bufs=1))
 
-        offs_sb = lists.tile([P, S // 16], U16, name="offs_sb")
-        two_sb = lists.tile([P, S // 16], U16, name="two_sb")
-        n1_sb = lists.tile([P, MEMBERS * S // 16], U16, name="n1_sb")
-        n2_sb = lists.tile([P, S // 16], U16, name="n2_sb")
-        n3_sb = lists.tile([P, S // 16], U16, name="n3_sb")
+        offs_sb = lists.tile([P, S // LIST], U16, name="offs_sb")
+        two_sb = lists.tile([P, S // LIST], U16, name="two_sb")
+        n1_sb = lists.tile([P, MEMBERS * S // LIST], U16, name="n1_sb")
+        n2_sb = lists.tile([P, S // LIST], U16, name="n2_sb")
+        n3_sb = lists.tile([P, S // LIST], U16, name="n3_sb")
 
-        table_words = keep.tile([P, T], U32, name="table_words")
-        table_scales = keep.tile([P, T], U8, name="table_scales")
-        nc.vector.memset(table_scales[:].bitcast(I32), 0)
         def load_columns(w, name, c0, c1):
             raw = keep.tile([P, PACK, c1 - c0], F32, name=f"{name}_raw{c0}")
             nc.sync.dma_start(raw[:], w.rearrange("(p j) c -> p j c", j=PACK)[:, :, c0:c1])
             return raw
 
+        table_words = keep.tile([P, T], U32, name="table_words")
+        table_scales = keep.tile([P, T], U8, name="table_scales")
+        nc.vector.memset(table_scales[:].bitcast(I32), 0)
         for q in range(4):
             queue = nc.sync if q < 2 else nc.scalar
             queue.dma_start(
@@ -80,7 +95,7 @@ def tile_picked_mixingsharehinge_none_p_kernel(tc, x_words, x_scales, w1, gn, w2
         nc.sync.dma_start(n2_sb[:], n2)
         nc.sync.dma_start(n3_sb[:], n3)
 
-        ex = [keep.tile([P, S + SPARE], F32, name=f"ex{t}") for t in range(PACK)]
+        ex = [keep.tile([P, S + EX_SPARE], F32, name=f"ex{t}") for t in range(PACK)]
         for t in range(PACK):
             nc.vector.memset(ex[t][:, S:], 0.0)
 
@@ -106,95 +121,6 @@ def tile_picked_mixingsharehinge_none_p_kernel(tc, x_words, x_scales, w1, gn, w2
                 out=words[:, c0:c1].bitcast(FP8X4), scales=scales[:, c0:c1], in_=grouped[:, PACK * c0 : PACK * c1]
             )
 
-        w1_mx, w2_mx, w3_mx = mx_tiles("w1", H), mx_tiles("w2", N), mx_tiles("w3", N)
-        weave("scalar", w1_mx[0], w1_raw[0], 0, 40, 0)
-        weave("vector", w1_mx[0], w1_raw[0], 40, 64, 0)
-        weave("vector", w1_mx[0], w1_raw[1], 64, 96, 64)
-        weave("scalar", w1_mx[0], w1_raw[2], 96, 106, 96)
-        weave("vector", w1_mx[0], w1_raw[2], 106, P, 96)
-
-        for t in range(PACK):
-            quantise(w1_mx, t * P, (t + 1) * P)
-        for t in range(PACK):
-            cols = slice(t * P, (t + 1) * P)
-            y = psum.tile([P, S], F32, name=f"y{t}", tag=f"bank{t}")
-            nc.tensor.matmul_mx(
-                out=y[:],
-                lhsT=w1_mx[1][:, cols].bitcast(FP8X4),
-                lhsT_scale=w1_mx[2][:, cols],
-                rhs=x1_words[:].bitcast(FP8X4),
-                rhs_scale=x1_scales[:],
-                start=True,
-                stop=True,
-            )
-            nc.scalar.activation(ex[t][:, :S], y[:], ACT.Exp, scale=0.5)
-
-        x2_words = keep.tile([P, S], U32, name="x2_words", tag="w1_bf16", align_bytes=64)
-        gather("vector", x2_words[:], table_words[:], two_sb[:])
-
-        h_sb = [keep.tile([P, S if t == PACK - 1 else 2 * S], F32, name=f"h_sb{t}") for t in range(PACK)]
-        for t in range(PACK - 1):
-            nc.vector.memset(h_sb[t][:, S:], 0.0)
-        front = [keep.tile([P, CHUNKS, MEMBERS * CHUNK], F32, name=f"front{t}") for t in range(2)]
-        back = [keep.tile([P, 2, MEMBERS * CHUNK], F32, name=f"back{c}") for c in range(CHUNKS)]
-        z_rows = keep.tile([P, PACK, S], BF16, name="z_rows")
-
-        def look_up(engine, t, c):
-            width = MEMBERS * CHUNK // 16
-            dst = front[t][:, c, :] if t < 2 else back[c][:, t - 2, :]
-            gather(engine, dst, ex[t][:], n1_sb[:, c * width : (c + 1) * width])
-
-        def inverse(out_ap, root, sums):
-            nc.scalar.activation(root, sums, ACT.Abs_reciprocal_sqrt, bias=0.125, scale=0.25)
-            nc.scalar.activation(out_ap, root, ACT.Square)
-
-        def scale(t, cols, recip):
-            nc.vector.scalar_tensor_tensor(
-                z_rows[:, t, cols], ex[t][:, cols], gn_sb[:, t : t + 1], recip, ALU.mult, ALU.mult
-            )
-
-        def front_rows(t):
-            sums = psum.tile([P, CHUNKS, P], F32, name=f"sums{t}", tag=f"bank{t}")
-            for c in range(CHUNKS):
-                planes = front[t][:, c, :].rearrange("p (j u) -> p u j", u=MEMBERS)
-                for u in range(MEMBERS):
-                    nc.tensor.matmul(
-                        sums[:, c, :], planes[:, u, :], identity[:],
-                        start=(u == 0), stop=(u == MEMBERS - 1), is_transpose=True,
-                    )
-            root = keep.tile([P, CHUNKS, P], F32, name=f"root{t}")
-            square = keep.tile([P, CHUNKS, P], F32, name=f"square{t}")
-            inverse(square[:], root[:], sums[:])
-            recip = psum.tile([P, S], F32, name=f"recip{t}", tag=f"bank{t}")
-            for c in range(CHUNKS):
-                nc.tensor.transpose(recip[:, c * CHUNK : (c + 1) * CHUNK], square[:, c, :], identity[:])
-            scale(t, slice(0, S), recip[:])
-
-        def back_rows(c, engine):
-            cols = slice(c * CHUNK, (c + 1) * CHUNK)
-            pairs = keep.tile([P, 2 * CHUNK, 2], F32, name=f"pairs{c}")
-            sums = keep.tile([P, 2 * CHUNK], F32, name=f"sums_sb{c}")
-            root = keep.tile([P, 2 * CHUNK], F32, name=f"root_sb{c}")
-            recip = keep.tile([P, 2, CHUNK], F32, name=f"recip_sb{c}")
-            four = back[c][:].rearrange("p t (j u) -> p (t j) u", u=MEMBERS)
-            engine.tensor_tensor(pairs[:], four[:, :, 0:2], four[:, :, 2:4], ALU.add)
-            engine.tensor_tensor(sums[:], pairs[:, :, 0], pairs[:, :, 1], ALU.add)
-            inverse(recip[:].rearrange("p t j -> p (t j)"), root[:], sums[:])
-            for i in range(2):
-                scale(2 + i, cols, recip[:, i, :])
-
-        def quantise_z(cols):
-            width = cols.stop - cols.start
-            z_mx = mx_tiles(f"z{cols.start}", width)
-            dst = z_mx[0][:].rearrange("p (j t) -> p j t", t=PACK)
-            src = z_rows[:, :, cols].rearrange("p t j -> p j t")
-            if cols.start // CHUNK in (1,):
-                nc.scalar.copy(dst, src)
-            else:
-                nc.vector.tensor_copy(dst, src)
-            quantise(z_mx, 0, width)
-            return z_mx
-
         def product(acc, w_mx, t, words, scales, start, stop):
             rows = slice(t * P, (t + 1) * P)
             nc.tensor.matmul_mx(
@@ -207,12 +133,91 @@ def tile_picked_mixingsharehinge_none_p_kernel(tc, x_words, x_scales, w1, gn, w2
                 stop=stop,
             )
 
-        def second_layer(cols, z_mx, tags):
-            width = cols.stop - cols.start
-            share = PACK // len(tags)
+        w1_mx, w2_mx, w3_mx = mx_tiles("w1", H), mx_tiles("w2", N), mx_tiles("w3", N)
+        (m0, m1), (m1, m2), (m2, m3) = [(c0 // PACK, c1 // PACK) for c0, c1 in W1_PIECES]
+        interleave_weight("scalar", w1_mx[0], w1_raw[0], m0, W1_CUT_FIRST, m0)
+        interleave_weight("vector", w1_mx[0], w1_raw[0], W1_CUT_FIRST, m1, m0)
+        interleave_weight("vector", w1_mx[0], w1_raw[1], m1, m2, m1)
+        interleave_weight("scalar", w1_mx[0], w1_raw[2], m2, W1_CUT_LAST, m2)
+        interleave_weight("vector", w1_mx[0], w1_raw[2], W1_CUT_LAST, m3, m2)
+        for t in range(PACK):
+            quantise(w1_mx, t * P, (t + 1) * P)
+        for t in range(PACK):
+            y = psum.tile([P, S], F32, name=f"y{t}", tag=f"bank{t}")
+            product(y[:], w1_mx, t, x1_words[:], x1_scales[:], True, True)
+            nc.scalar.activation(ex[t][:, :S], y[:], ACT.Exp, scale=0.5)
+
+        x2_words = keep.tile([P, S], U32, name="x2_words", tag="w1_bf16", align_bytes=64)
+        gather("vector", x2_words[:], table_words[:], two_sb[:])
+
+        h_sb = [keep.tile([P, S if t == PACK - 1 else 2 * S], F32, name=f"h_sb{t}") for t in range(PACK)]
+        for t in range(PACK - 1):
+            nc.vector.memset(h_sb[t][:, S:], 0.0)
+
+        front = [keep.tile([P, CHUNKS, MEMBERS * CHUNK], F32, name=f"front{t}") for t in range(FRONT)]
+        back = [keep.tile([P, PACK - FRONT, MEMBERS * CHUNK], F32, name=f"back{c}") for c in range(CHUNKS)]
+        z_rows = keep.tile([P, PACK, S], BF16, name="z_rows")
+
+        def look_up(engine, dst, t, c):
+            entries = slice(c * MEMBERS * CHUNK, (c + 1) * MEMBERS * CHUNK)
+            gather(engine, dst, ex[t][:], n1_sb[:, list_columns(entries)])
+
+        def inverse(result, root, sums):
+            nc.scalar.activation(root, sums, ACT.Abs_reciprocal_sqrt, bias=0.125, scale=0.25)
+            nc.scalar.activation(result, root, ACT.Square)
+
+        def make_z(t, cols, recip):
+            nc.vector.scalar_tensor_tensor(
+                z_rows[:, t, cols], ex[t][:, cols], gn_sb[:, t : t + 1], recip, ALU.mult, ALU.mult
+            )
+
+        def front_rows(t):
+            sums = psum.tile([P, CHUNKS, P], F32, name=f"sums{t}", tag=f"bank{t}")
+            for c in range(CHUNKS):
+                by_member = front[t][:, c, :].rearrange("p (j u) -> p u j", u=MEMBERS)
+                for u in range(MEMBERS):
+                    nc.tensor.matmul(
+                        sums[:, c, :], by_member[:, u, :], identity[:],
+                        start=(u == 0), stop=(u == MEMBERS - 1), is_transpose=True,
+                    )
+            root = keep.tile([P, CHUNKS, P], F32, name=f"root{t}")
+            square = keep.tile([P, CHUNKS, P], F32, name=f"square{t}")
+            inverse(square[:], root[:], sums[:])
+            recip = psum.tile([P, S], F32, name=f"recip{t}", tag=f"bank{t}")
+            for c in range(CHUNKS):
+                nc.tensor.transpose(recip[:, chunk_columns(c)], square[:, c, :], identity[:])
+            make_z(t, slice(0, S), recip[:])
+
+        def back_rows(c):
+            width = (PACK - FRONT) * CHUNK
+            pairs = keep.tile([P, width, 2], F32, name=f"pairs{c}")
+            sums = keep.tile([P, width], F32, name=f"sums_sb{c}")
+            root = keep.tile([P, width], F32, name=f"root_sb{c}")
+            recip = keep.tile([P, PACK - FRONT, CHUNK], F32, name=f"recip_sb{c}")
+            four = back[c][:].rearrange("p t (j u) -> p (t j) u", u=MEMBERS)
+            nc.vector.tensor_tensor(pairs[:], four[:, :, 0:2], four[:, :, 2:4], ALU.add)
+            nc.vector.tensor_tensor(sums[:], pairs[:, :, 0], pairs[:, :, 1], ALU.add)
+            inverse(recip[:].rearrange("p t j -> p (t j)"), root[:], sums[:])
+            for i in range(PACK - FRONT):
+                make_z(FRONT + i, chunk_columns(c), recip[:, i, :])
+
+        def quantise_z(c):
+            z_mx = mx_tiles(f"z{c * CHUNK}", CHUNK)
+            dst = z_mx[0][:].rearrange("p (j t) -> p j t", t=PACK)
+            src = z_rows[:, :, chunk_columns(c)].rearrange("p t j -> p j t")
+            if c == Z_CHUNK_ON_SCALAR:
+                nc.scalar.copy(dst, src)
+            else:
+                nc.vector.tensor_copy(dst, src)
+            quantise(z_mx, 0, CHUNK)
+            return z_mx
+
+        def second_layer(c, z_mx, banks):
+            cols = chunk_columns(c)
+            share = PACK // len(banks)
             sums = []
-            for b, tag in enumerate(tags):
-                bank = psum.tile([P, share, width], F32, name=f"h{cols.start}_{b}", tag=tag)
+            for b, tag in enumerate(banks):
+                bank = psum.tile([P, share, CHUNK], F32, name=f"h{c * CHUNK}_{b}", tag=tag)
                 for i in range(share):
                     product(bank[:, i, :], w3_mx, b * share + i, x2_words[:, cols], x2_scales[:, cols], i == 0, False)
                 for i in range(share):
@@ -220,42 +225,40 @@ def tile_picked_mixingsharehinge_none_p_kernel(tc, x_words, x_scales, w1, gn, w2
                     sums.append(bank[:, i, :])
             return sums
 
-        def copy_out(t, cols, sums):
-            if cols.start // CHUNK in (2,):
-                nc.vector.tensor_copy(h_sb[t][:, cols], sums[t])
+        def copy_out(t, c, sums):
+            if c == H_CHUNK_ON_VECTOR:
+                nc.vector.tensor_copy(h_sb[t][:, chunk_columns(c)], sums[t])
             else:
-                nc.scalar.activation(h_sb[t][:, cols], sums[t], ACT.Copy)
+                nc.scalar.activation(h_sb[t][:, chunk_columns(c)], sums[t], ACT.Copy)
 
-        def prepare(w_mx, w_raw):
-            for part in range(4):
-                weave("gpsimd", w_mx[0], w_raw, 32 * part, 32 * (part + 1), 0)
-            quantise(w_mx, 0, S)
+        def prepare_weight(w_mx, w_raw):
+            part = P // GPSIMD_PARTS
+            for i in range(GPSIMD_PARTS):
+                interleave_weight("gpsimd", w_mx[0], w_raw, part * i, part * (i + 1), 0)
+            quantise(w_mx, 0, N)
 
-        last = slice(S - CHUNK, S)
-        for t in range(2):
+        for t in range(FRONT):
             for c in range(CHUNKS):
-                look_up("vector", t, c)
+                look_up("vector", front[t][:, c, :], t, c)
         for c in range(CHUNKS):
-            for t in (2, 3):
-                look_up("vector" if (c, t) == (3, 2) else "scalar", t, c)
-        prepare(w3_mx, w3_raw)
-        prepare(w2_mx, w2_raw)
-        for t in range(2):
+            for t in range(FRONT, PACK):
+                look_up("scalar", back[c][:, t - FRONT, :], t, c)
+        prepare_weight(w3_mx, w3_raw)
+        prepare_weight(w2_mx, w2_raw)
+        for t in range(FRONT):
             front_rows(t)
         h_psum = []
         for c in range(CHUNKS):
-            cols = slice(c * CHUNK, (c + 1) * CHUNK)
-            back_rows(c, nc.gpsimd if c < 2 else nc.vector)
-            tags = (f"bank{c}",) if c < CHUNKS - 1 else ("bank4", "bank5", "bank6", "bank7")
-            h_psum.append(second_layer(cols, quantise_z(cols), tags))
+            back_rows(c)
+            banks = (f"bank{c}",) if c < CHUNKS - 1 else tuple(f"bank{PACK + t}" for t in range(PACK))
+            h_psum.append(second_layer(c, quantise_z(c), banks))
         for c in range(CHUNKS - 1):
             for t in range(PACK):
-                copy_out(t, slice(c * CHUNK, (c + 1) * CHUNK), h_psum[c])
-        h_last = h_psum[-1]
+                copy_out(t, c, h_psum[c])
 
         out_rows = out.rearrange("(p t) n -> p t n", t=PACK)
         for t in range(PACK):
-            copy_out(t, last, h_last)
+            copy_out(t, CHUNKS - 1, h_psum[-1])
             at2 = keep.tile([P, S], F32, name=f"at2_{t}")
             at3 = keep.tile([P, S], F32, name=f"at3_{t}")
             down = keep.tile([P, S], F32, name=f"down{t}")
@@ -263,14 +266,13 @@ def tile_picked_mixingsharehinge_none_p_kernel(tc, x_words, x_scales, w1, gn, w2
             up_half = keep.tile([P, S], F32, name=f"up_half{t}")
             result = keep.tile([P, S], F32, name=f"result{t}")
             h = h_sb[t][:, :S]
-            halves = [slice(0, S)] if t < PACK - 1 else [slice(0, HALF), slice(HALF, S)]
-            for cols in halves:
-                gather("vector" if t == 0 else "scalar", at3[:, cols], h_sb[t][:], n3_sb[:, cols.start // 16 : cols.stop // 16])
+            spans = [slice(0, S)] if t < PACK - 1 else [slice(0, HALF), slice(HALF, S)]
+            for cols in spans:
+                gather("vector" if t == 0 else "scalar", at3[:, cols], h_sb[t][:], n3_sb[:, list_columns(cols)])
                 nc.vector.tensor_tensor(up[:, cols], at3[:, cols], h[:, cols], ALU.subtract)
                 nc.vector.tensor_scalar(up_half[:, cols], up[:, cols], 0.0, 0.5, ALU.max, ALU.mult)
-            spans = [slice(0, S)] if t < PACK - 1 else halves
             for cols in spans:
-                gather("scalar", at2[:, cols], h_sb[t][:], n2_sb[:, cols.start // 16 : cols.stop // 16])
+                gather("scalar", at2[:, cols], h_sb[t][:], n2_sb[:, list_columns(cols)])
                 nc.vector.tensor_tensor(down[:, cols], h[:, cols], at2[:, cols], ALU.subtract)
                 nc.vector.scalar_tensor_tensor(result[:, cols], down[:, cols], 0.0, up_half[:, cols], ALU.max, ALU.add)
                 nc.sync.dma_start(out_rows[:, t, cols], result[:, cols])

from contextlib import ExitStack

import concourse.mybir as mybir
from concourse.masks import make_identity

F32 = mybir.dt.float32
BF16 = mybir.dt.bfloat16
I32 = mybir.dt.int32
U32 = mybir.dt.uint32
U16 = mybir.dt.uint16
U8 = mybir.dt.uint8
FP8X4 = mybir.dt.float8_e4m3fn_x4
ALU = mybir.AluOpType
ACT = mybir.ActivationFunctionType

P = 128
PACK = 4
T, S, H, N = 2048, 512, 512, 512
MEMBERS = 4
LIST = 16
CHUNK = 128
CHUNKS = S // CHUNK
HALF = S // 2
FRONT = 2
EX_SPARE = 32

W1_PIECES = ((0, 256), (256, 384), (384, 512))
W1_CUT_FIRST, W1_CUT_LAST = 40, 106
GPSIMD_PARTS = 4
Z_CHUNK_ON_SCALAR, H_CHUNK_ON_VECTOR = 1, 2

FLOPS = 3 * 2 * 512 * 512 * 512


def tile_picked_mixingsharehinge_none_p_kernel(
    tc, x_words, x_scales, w1, gn, w2, w3, offs, n1, two, n2, n3, out
):
    nc = tc.nc

    def gather(engine, dst, window, offsets):
        if engine == "vector":
            nc.vector.tensor_copy(dst, window.indirect(offsets))
        else:
            nc.scalar.activation(dst, window.indirect(offsets), ACT.Copy)

    def interleave_weight(engine, grouped, raw, m0, m1, raw_m0):
        dst = grouped[:].rearrange("p (t m j) -> p m t j", t=PACK, j=PACK)[:, m0:m1]
        src = raw[:].rearrange("p j (m t) -> p m t j", t=PACK)[:, m0 - raw_m0 : m1 - raw_m0]
        if engine == "vector":
            nc.vector.tensor_copy(dst, src)
        elif engine == "gpsimd":
            nc.gpsimd.tensor_scalar(dst, src, 1.0, 0.0, ALU.mult, ALU.add)
        else:
            nc.scalar.activation(dst, src, ACT.Copy)

    def chunk_columns(c):
        return slice(c * CHUNK, (c + 1) * CHUNK)

    def list_columns(entries):
        return slice(entries.start // LIST, entries.stop // LIST)

    with ExitStack() as ctx:
        lists = ctx.enter_context(tc.tile_pool(name="lists", bufs=1))
        keep = ctx.enter_context(tc.tile_pool(name="keep", bufs=1))
        psum = ctx.enter_context(tc.psum_pool(name="psum", bufs=1))

        offs_sb = lists.tile([P, S // LIST], U16, name="offs_sb")
        two_sb = lists.tile([P, S // LIST], U16, name="two_sb")
        n1_sb = lists.tile([P, MEMBERS * S // LIST], U16, name="n1_sb")
        n2_sb = lists.tile([P, S // LIST], U16, name="n2_sb")
        n3_sb = lists.tile([P, S // LIST], U16, name="n3_sb")

        def load_columns(w, name, c0, c1):
            raw = keep.tile([P, PACK, c1 - c0], F32, name=f"{name}_raw{c0}")
            nc.sync.dma_start(raw[:], w.rearrange("(p j) c -> p j c", j=PACK)[:, :, c0:c1])
            return raw

        table_words = keep.tile([P, T], U32, name="table_words")
        table_scales = keep.tile([P, T], U8, name="table_scales")
        nc.vector.memset(table_scales[:].bitcast(I32), 0)
        for q in range(4):
            queue = nc.sync if q < 2 else nc.scalar
            queue.dma_start(
                table_scales[32 * q : 32 * q + 4, :].bitcast(I32), x_scales[0, 4 * q : 4 * q + 4, :].bitcast(I32)
            )
        nc.sync.dma_start(offs_sb[:], offs)
        nc.sync.dma_start(two_sb[:], two)
        nc.sync.dma_start(table_words[:].bitcast(I32), x_words[0].rearrange("p n t -> p (n t)").bitcast(I32))
        w1_raw = [load_columns(w1, "w1", c0, c1) for c0, c1 in W1_PIECES]
        nc.sync.dma_start(n1_sb[:], n1)
        gn_sb = keep.tile([P, PACK], F32, name="gn_sb")
        nc.sync.dma_start(gn_sb[:], gn.rearrange("(p t) o -> p (t o)", t=PACK))
        w3_raw = load_columns(w3, "w3", 0, N)
        w2_raw = load_columns(w2, "w2", 0, N)
        nc.sync.dma_start(n2_sb[:], n2)
        nc.sync.dma_start(n3_sb[:], n3)

        ex = [keep.tile([P, S + EX_SPARE], F32, name=f"ex{t}") for t in range(PACK)]
        for t in range(PACK):
            nc.vector.memset(ex[t][:, S:], 0.0)

        identity = keep.tile([P, P], F32, name="identity")
        make_identity(nc, identity[:])

        x1_words = keep.tile([P, S], U32, name="x1_words", align_bytes=64)
        x1_scales = keep.tile([P, S], U8, name="x1_scales", align_bytes=64)
        x2_scales = keep.tile([P, S], U8, name="x2_scales", align_bytes=64)
        gather("vector", x1_scales[:], table_scales[:], offs_sb[:])
        gather("vector", x2_scales[:], table_scales[:], two_sb[:])
        gather("vector", x1_words[:], table_words[:], offs_sb[:])

        def mx_tiles(name, width):
            grouped = keep.tile([P, PACK * width], BF16, name=name + "_bf16", tag=name + "_bf16", align_bytes=64)
            words = keep.tile([P, width], U32, name=name + "_words", align_bytes=64)
            scales = keep.tile([P, width], U8, name=name + "_scales", align_bytes=64)
            return grouped, words, scales

        def quantise(tiles, c0, c1):
            grouped, words, scales = tiles
            nc.vector.quantize_mx(
                out=words[:, c0:c1].bitcast(FP8X4), scales=scales[:, c0:c1], in_=grouped[:, PACK * c0 : PACK * c1]
            )

        def product(acc, w_mx, t, words, scales, start, stop):
            rows = slice(t * P, (t + 1) * P)
            nc.tensor.matmul_mx(
                out=acc,
                lhsT=w_mx[1][:, rows].bitcast(FP8X4),
                lhsT_scale=w_mx[2][:, rows],
                rhs=words.bitcast(FP8X4),
                rhs_scale=scales,
                start=start,
                stop=stop,
            )

        w1_mx, w2_mx, w3_mx = mx_tiles("w1", H), mx_tiles("w2", N), mx_tiles("w3", N)
        (m0, m1), (m1, m2), (m2, m3) = [(c0 // PACK, c1 // PACK) for c0, c1 in W1_PIECES]
        interleave_weight("scalar", w1_mx[0], w1_raw[0], m0, W1_CUT_FIRST, m0)
        interleave_weight("vector", w1_mx[0], w1_raw[0], W1_CUT_FIRST, m1, m0)
        interleave_weight("vector", w1_mx[0], w1_raw[1], m1, m2, m1)
        interleave_weight("scalar", w1_mx[0], w1_raw[2], m2, W1_CUT_LAST, m2)
        interleave_weight("vector", w1_mx[0], w1_raw[2], W1_CUT_LAST, m3, m2)
        for t in range(PACK):
            quantise(w1_mx, t * P, (t + 1) * P)
        for t in range(PACK):
            y = psum.tile([P, S], F32, name=f"y{t}", tag=f"bank{t}")
            product(y[:], w1_mx, t, x1_words[:], x1_scales[:], True, True)
            nc.scalar.activation(ex[t][:, :S], y[:], ACT.Exp, scale=0.5)

        x2_words = keep.tile([P, S], U32, name="x2_words", tag="w1_bf16", align_bytes=64)
        gather("vector", x2_words[:], table_words[:], two_sb[:])

        h_sb = [keep.tile([P, S if t == PACK - 1 else 2 * S], F32, name=f"h_sb{t}") for t in range(PACK)]
        for t in range(PACK - 1):
            nc.vector.memset(h_sb[t][:, S:], 0.0)

        front = [keep.tile([P, CHUNKS, MEMBERS * CHUNK], F32, name=f"front{t}") for t in range(FRONT)]
        back = [keep.tile([P, PACK - FRONT, MEMBERS * CHUNK], F32, name=f"back{c}") for c in range(CHUNKS)]
        z_rows = keep.tile([P, PACK, S], BF16, name="z_rows")

        def look_up(engine, dst, t, c):
            entries = slice(c * MEMBERS * CHUNK, (c + 1) * MEMBERS * CHUNK)
            gather(engine, dst, ex[t][:], n1_sb[:, list_columns(entries)])

        def inverse(result, root, sums):
            nc.scalar.activation(root, sums, ACT.Abs_reciprocal_sqrt, bias=0.125, scale=0.25)
            nc.scalar.activation(result, root, ACT.Square)

        def make_z(t, cols, recip):
            nc.vector.scalar_tensor_tensor(
                z_rows[:, t, cols], ex[t][:, cols], gn_sb[:, t : t + 1], recip, ALU.mult, ALU.mult
            )

        def front_rows(t):
            sums = psum.tile([P, CHUNKS, P], F32, name=f"sums{t}", tag=f"bank{t}")
            for c in range(CHUNKS):
                by_member = front[t][:, c, :].rearrange("p (j u) -> p u j", u=MEMBERS)
                for u in range(MEMBERS):
                    nc.tensor.matmul(
                        sums[:, c, :], by_member[:, u, :], identity[:],
                        start=(u == 0), stop=(u == MEMBERS - 1), is_transpose=True,
                    )
            root = keep.tile([P, CHUNKS, P], F32, name=f"root{t}")
            square = keep.tile([P, CHUNKS, P], F32, name=f"square{t}")
            inverse(square[:], root[:], sums[:])
            recip = psum.tile([P, S], F32, name=f"recip{t}", tag=f"bank{t}")
            for c in range(CHUNKS):
                nc.tensor.transpose(recip[:, chunk_columns(c)], square[:, c, :], identity[:])
            make_z(t, slice(0, S), recip[:])

        def back_rows(c):
            width = (PACK - FRONT) * CHUNK
            pairs = keep.tile([P, width, 2], F32, name=f"pairs{c}")
            sums = keep.tile([P, width], F32, name=f"sums_sb{c}")
            root = keep.tile([P, width], F32, name=f"root_sb{c}")
            recip = keep.tile([P, PACK - FRONT, CHUNK], F32, name=f"recip_sb{c}")
            four = back[c][:].rearrange("p t (j u) -> p (t j) u", u=MEMBERS)
            nc.vector.tensor_tensor(pairs[:], four[:, :, 0:2], four[:, :, 2:4], ALU.add)
            nc.vector.tensor_tensor(sums[:], pairs[:, :, 0], pairs[:, :, 1], ALU.add)
            inverse(recip[:].rearrange("p t j -> p (t j)"), root[:], sums[:])
            for i in range(PACK - FRONT):
                make_z(FRONT + i, chunk_columns(c), recip[:, i, :])

        def quantise_z(c):
            z_mx = mx_tiles(f"z{c * CHUNK}", CHUNK)
            dst = z_mx[0][:].rearrange("p (j t) -> p j t", t=PACK)
            src = z_rows[:, :, chunk_columns(c)].rearrange("p t j -> p j t")
            if c == Z_CHUNK_ON_SCALAR:
                nc.scalar.copy(dst, src)
            else:
                nc.vector.tensor_copy(dst, src)
            quantise(z_mx, 0, CHUNK)
            return z_mx

        def second_layer(c, z_mx, banks):
            cols = chunk_columns(c)
            share = PACK // len(banks)
            sums = []
            for b, tag in enumerate(banks):
                bank = psum.tile([P, share, CHUNK], F32, name=f"h{c * CHUNK}_{b}", tag=tag)
                for i in range(share):
                    product(bank[:, i, :], w3_mx, b * share + i, x2_words[:, cols], x2_scales[:, cols], i == 0, False)
                for i in range(share):
                    product(bank[:, i, :], w2_mx, b * share + i, z_mx[1][:], z_mx[2][:], False, i == share - 1)
                    sums.append(bank[:, i, :])
            return sums

        def copy_out(t, c, sums):
            if c == H_CHUNK_ON_VECTOR:
                nc.vector.tensor_copy(h_sb[t][:, chunk_columns(c)], sums[t])
            else:
                nc.scalar.activation(h_sb[t][:, chunk_columns(c)], sums[t], ACT.Copy)

        def prepare_weight(w_mx, w_raw):
            part = P // GPSIMD_PARTS
            for i in range(GPSIMD_PARTS):
                interleave_weight("gpsimd", w_mx[0], w_raw, part * i, part * (i + 1), 0)
            quantise(w_mx, 0, N)

        for t in range(FRONT):
            for c in range(CHUNKS):
                look_up("vector", front[t][:, c, :], t, c)
        for c in range(CHUNKS):
            for t in range(FRONT, PACK):
                look_up("scalar", back[c][:, t - FRONT, :], t, c)
        prepare_weight(w3_mx, w3_raw)
        prepare_weight(w2_mx, w2_raw)
        for t in range(FRONT):
            front_rows(t)
        h_psum = []
        for c in range(CHUNKS):
            back_rows(c)
            banks = (f"bank{c}",) if c < CHUNKS - 1 else tuple(f"bank{PACK + t}" for t in range(PACK))
            h_psum.append(second_layer(c, quantise_z(c), banks))
        for c in range(CHUNKS - 1):
            for t in range(PACK):
                copy_out(t, c, h_psum[c])

        out_rows = out.rearrange("(p t) n -> p t n", t=PACK)
        for t in range(PACK):
            copy_out(t, CHUNKS - 1, h_psum[-1])
            at2 = keep.tile([P, S], F32, name=f"at2_{t}")
            at3 = keep.tile([P, S], F32, name=f"at3_{t}")
            down = keep.tile([P, S], F32, name=f"down{t}")
            up = keep.tile([P, S], F32, name=f"up{t}")
            up_half = keep.tile([P, S], F32, name=f"up_half{t}")
            result = keep.tile([P, S], F32, name=f"result{t}")
            h = h_sb[t][:, :S]
            spans = [slice(0, S)] if t < PACK - 1 else [slice(0, HALF), slice(HALF, S)]
            for cols in spans:
                gather("vector" if t == 0 else "scalar", at3[:, cols], h_sb[t][:], n3_sb[:, list_columns(cols)])
                nc.vector.tensor_tensor(up[:, cols], at3[:, cols], h[:, cols], ALU.subtract)
                nc.vector.tensor_scalar(up_half[:, cols], up[:, cols], 0.0, 0.5, ALU.max, ALU.mult)
            for cols in spans:
                gather("scalar", at2[:, cols], h_sb[t][:], n2_sb[:, list_columns(cols)])
                nc.vector.tensor_tensor(down[:, cols], h[:, cols], at2[:, cols], ALU.subtract)
                nc.vector.scalar_tensor_tensor(result[:, cols], down[:, cols], 0.0, up_half[:, cols], ALU.max, ALU.add)
                nc.sync.dma_start(out_rows[:, t, cols], result[:, cols])
